import numpy as np
import ml_dtypes


def mxq(x, axis, fmt="e4m3"):
    dtype, down = {"e4m3": (ml_dtypes.float8_e4m3fn, 7), "e5m2": (ml_dtypes.float8_e5m2, 14)}[fmt]
    v = np.moveaxis(np.asarray(x, np.float32).astype(ml_dtypes.bfloat16).astype(np.float64), axis, -1)
    blocks = v.reshape(v.shape[:-1] + (-1, 32))
    amax = np.abs(blocks).max(-1, keepdims=True)
    byte = np.maximum(np.where(amax > 0, np.frexp(amax)[1] - 1 + 127, 0) - down, 1)
    scale = np.exp2(byte - 127.0)
    codes = (blocks / scale).astype(np.float32).astype(dtype).astype(np.float64)
    return np.moveaxis((codes * scale).reshape(v.shape), -1, axis)


WIDE = False


def mx_kscale(k):
    if not WIDE:
        return np.ones(k)
    levels = np.array([10, -10, 5, -5, 0])
    if k % 512:
        return np.exp2(np.random.permutation(np.resize(levels, k // 32))).repeat(32)
    a = np.empty((k // 512, 16))
    for p in range(k // 512):
        a[p, :8] = np.random.permutation(np.resize(levels, 8))
        for g in range(8):
            far = levels[np.abs(levels - a[p, g]) >= 10]
            a[p, g + 8] = far[np.random.randint(len(far))]
    return np.exp2(a.ravel()).repeat(32)


def f64(x):
    return np.asarray(x).astype(np.float64)


def striped8(idx):
    return np.concatenate([v.reshape(-1, 16).T for v in idx]).astype(np.uint16)


def unstriped8(offs):
    return np.stack([offs[16 * g:16 * g + 16].T.reshape(-1) for g in range(8)]).astype(np.int64)


E2M1 = np.array([0.0, 0.5, 1.0, 1.5, 2.0, 3.0, 4.0, 6.0, -0.0, -0.5, -1.0, -1.5, -2.0, -3.0, -4.0, -6.0])


def pack_weight(w, fmt):
    k, n = w.shape
    w = f64(np.asarray(w, np.float32).astype(ml_dtypes.bfloat16)).reshape(k // 32, 32, n)
    amax = np.abs(w).max(1)
    if fmt == "e4m3":
        byte = np.frexp(amax)[1] - 1 + 127 - 7
    else:
        mant, ex = np.frexp(amax / 6.0)
        byte = np.where(mant > 0.5, ex, ex - 1) + 127
    byte = np.clip(np.where(amax > 0, byte, 1), 1, 254)
    scaled = (w * np.exp2(127.0 - byte)[:, None, :]).reshape(k, n).astype(np.float32)
    by_word = np.ascontiguousarray(scaled.reshape(k // 512, 128, 4, n).transpose(0, 1, 3, 2))
    if fmt == "e4m3":
        words = by_word.astype(ml_dtypes.float8_e4m3fn).view(np.uint8)
    else:
        c = by_word.astype(ml_dtypes.float4_e2m1fn).view(np.uint8) & 0xF
        words = (c[..., 0::2] | (c[..., 1::2] << 4)).reshape(k // 512, 128, 2 * n)
    return np.ascontiguousarray(words), np.ascontiguousarray(byte.astype(np.uint8).reshape(k // 512, 16, n))


def unpack_weight(words, scales, fmt):
    g, _, n = scales.shape
    words = np.ascontiguousarray(words).reshape(g, 128, n, -1)
    if fmt == "e4m3":
        vals = words.view(ml_dtypes.float8_e4m3fn).astype(np.float64)
    else:
        nib = np.empty((g, 128, n, 4), np.uint8)
        nib[..., 0::2] = words & 0xF
        nib[..., 1::2] = words >> 4
        vals = E2M1[nib]
    vals = vals * np.repeat(np.exp2(scales.astype(np.float64) - 127.0), 8, axis=1)[..., None]
    return vals.transpose(0, 1, 3, 2).reshape(g * 512, n)


def gelu(v):
    return 0.5 * v * (1.0 + np.tanh(np.sqrt(2.0 / np.pi) * (v + 0.044715 * v**3)))


K, M, T, S = 512, 1024, 1024, 512


def setup_inputs():
    n = np.random.standard_normal
    s = mx_kscale(K)[:, None]
    p_w = pack_weight(n((K, M)) / np.sqrt(K) / s, "e2m1")
    return {
        "xT": (n((K, T)) * s).astype(np.float32),
        "w_words": p_w[0],
        "w_scales": p_w[1],
        "wgt": np.repeat(np.random.uniform(0.5, 2.0, (8, S)), 16, axis=0).astype(np.float32),
        "b": (0.3 * n(1024)).astype(np.float32),
        "wgo": np.repeat(np.random.uniform(0.5, 2.0, (8, S)), 16, axis=0).astype(np.float32),
        "offs": striped8(np.stack([np.random.permutation(T)[:S] for _ in range(8)])),
        "offs2": striped8(np.stack([np.random.permutation(T)[:S] for _ in range(8)])),
    }


def reference(xT, w_words, w_scales, wgt, b, wgo, offs, offs2):
    idx = unstriped8(offs)
    group = np.arange(K) % 512 // 64
    xg = f64(wgt)[np.arange(K) // 4 % 128] * f64(xT)[np.arange(K)[:, None], idx[group]]
    xT_ = mxq(xg, 0, "e4m3")
    w_ = unpack_weight(w_words, w_scales, "e2m1")
    y = w_.T @ xT_
    place = unstriped8(offs2)[np.arange(M) % 128 // 16]
    out = np.zeros((M, T))
    out[np.arange(M)[:, None], place] = f64(wgo)[np.arange(M) % 128] * (gelu(y + f64(b)[:, None]))
    return out

@@ -1,0 +1,138 @@
+from contextlib import ExitStack
+
+import concourse.mybir as mybir
+
+K, M, T, S = 512, 1024, 1024, 512
+P = 128
+PACK = 4
+HALF = S // 2
+M_TILES = M // P
+FLOPS = 2 * K * M * S
+
+F32 = mybir.dt.float32
+BF16 = mybir.dt.bfloat16
+I32 = mybir.dt.int32
+U32 = mybir.dt.uint32
+U16 = mybir.dt.uint16
+U8 = mybir.dt.uint8
+FP8X4 = mybir.dt.float8_e4m3fn_x4
+FP4X4 = mybir.dt.float4_e2m1fn_x4
+MULT = mybir.AluOpType.mult
+GELU = mybir.ActivationFunctionType.Gelu_apprx_tanh
+
+
+def tile_list_hboth_gelu_kernel(tc, xT, w_words, w_scales, wgt, b, wgo, offs, offs2, out):
+    nc = tc.nc
+    with ExitStack() as ctx:
+        lists = ctx.enter_context(tc.tile_pool(name="lists", bufs=1))
+        keep = ctx.enter_context(tc.tile_pool(name="keep", bufs=1))
+        psum = ctx.enter_context(tc.psum_pool(name="psum", bufs=8))
+
+        picks = lists.tile([P, S // 16], U16, name="picks")
+        places = lists.tile([P, S // 16], U16, name="places")
+        wgt_half = [keep.tile([P, HALF], F32, name=f"wgt{h}") for h in range(2)]
+        planes = [keep.tile([P, T], F32, name=f"plane{i}") for i in range(PACK)]
+        w_codes = keep.tile([P, 2 * M], U8, name="w_codes", align_bytes=64)
+        w_plane = keep.tile([P, M], U8, name="w_plane", align_bytes=64)
+        wgo_all = keep.tile([P, S], F32, name="wgo_all")
+        b_rows = keep.tile([P, 32], F32, name="b_rows", align_bytes=64)
+        b_cols = keep.tile([P, 32], F32, name="b_cols", align_bytes=64)
+        warm_in = keep.tile([P, 8], F32, name="warm_in")
+        warm_out = keep.tile([P, 8], F32, name="warm_out")
+        rows = [keep.tile([P, T], F32, name=f"rows{m}") for m in range(M_TILES)]
+
+        nc.vector.memset(w_plane[:].bitcast(I32), 0)
+        nc.vector.memset(b_rows[:], 0.0)
+        nc.vector.memset(warm_in[:], 0.0)
+        nc.scalar.activation(warm_out[:], warm_in[:], GELU)
+
+        x_planes = xT.rearrange("(p i) t -> p i t", i=PACK)
+        nc.sync.dma_start(picks[:], offs)
+        nc.sync.dma_start(out=wgt_half[0][:], in_=wgt[:, 0:HALF])
+        nc.sync.dma_start(out=planes[0][:], in_=x_planes[:, 0, :])
+        nc.sync.dma_start(out=wgt_half[1][:], in_=wgt[:, HALF:S])
+        for i in range(1, PACK):
+            nc.sync.dma_start(out=planes[i][:], in_=x_planes[:, i, :])
+        for q in range(4):
+            nc.scalar.dma_start(
+                out=w_plane[32 * q : 32 * q + 4, :].bitcast(I32),
+                in_=w_scales[0, 4 * q : 4 * q + 4, :].bitcast(I32),
+            )
+        b_view = b.rearrange("(m q c) -> q m c", q=4, c=32)
+        for q in range(4):
+            nc.scalar.dma_start(out=b_rows[32 * q : 32 * q + M_TILES, :], in_=b_view[q])
+        nc.sync.dma_start(out=w_codes[:].bitcast(I32), in_=w_words[0].bitcast(I32))
+        nc.sync.dma_start(places[:], offs2)
+        nc.sync.dma_start(out=wgo_all[:], in_=wgo)
+
+        for m in range(M_TILES):
+            if m < 5:
+                nc.vector.memset(rows[m][:], 0.0)
+            else:
+                nc.gpsimd.memset(rows[m][:], 0.0)
+        nc.vector.transpose(b_cols[:], b_rows[:])
+
+        codes = keep.tile([P, S], U32, name="codes", align_bytes=64)
+        scales = keep.tile([P, S], U8, name="scales", align_bytes=64)
+        picked = [keep.tile([P, PACK, HALF], F32, name=f"picked{h}") for h in range(2)]
+        grouped = [keep.tile([P, HALF, PACK], BF16, name=f"grouped{h}", align_bytes=64) for h in range(2)]
+        results = [[keep.tile([P, HALF], F32, name=f"res{m}_{h}") for h in range(2)] for m in range(M_TILES)]
+
+        def gather(h):
+            lo = h * HALF // 16
+            for i in range(PACK):
+                nc.vector.tensor_tensor(
+                    picked[h][:, i, :],
+                    planes[i][:].indirect(picks[:, lo : lo + HALF // 16]),
+                    wgt_half[h][:],
+                    MULT,
+                )
+                if i % 2 == 1:
+                    nc.scalar.copy(
+                        out=grouped[h][:, :, i - 1 : i + 1],
+                        in_=picked[h][:, i - 1 : i + 1, :].rearrange("p t c -> p c t"),
+                    )
+
+        def quantize(h):
+            cols = slice(h * HALF, (h + 1) * HALF)
+            nc.vector.quantize_mx(
+                out=codes[:, cols].bitcast(FP8X4),
+                scales=scales[:, cols],
+                in_=grouped[h][:].rearrange("p c t -> p (c t)"),
+            )
+
+        def project(m, h):
+            cols = slice(h * HALF, (h + 1) * HALF)
+            acc = psum.tile([P, HALF], F32, name="acc")
+            nc.tensor.matmul_mx(
+                out=acc[:],
+                lhsT=w_codes[:, 2 * P * m : 2 * P * (m + 1)].bitcast(FP4X4),
+                lhsT_scale=w_plane[:, P * m : P * (m + 1)],
+                rhs=codes[:, cols].bitcast(FP8X4),
+                rhs_scale=scales[:, cols],
+                start=True,
+                stop=True,
+            )
+            nc.scalar.activation(results[m][h][:], acc[:], GELU, bias=b_cols[:, m : m + 1])
+            lo = h * HALF // 16
+            nc.vector.tensor_tensor(
+                rows[m][:].indirect(places[:, lo : lo + HALF // 16]),
+                results[m][h][:],
+                wgo_all[:, cols],
+                MULT,
+            )
+
+        def store(m):
+            nc.sync.dma_start(out=out[P * m : P * (m + 1), :], in_=rows[m][:])
+
+        gather(0)
+        quantize(0)
+        project(0, 0)
+        gather(1)
+        quantize(1)
+        project(1, 0)
+        for m in range(M_TILES):
+            if m >= 2:
+                project(m, 0)
+            project(m, 1)
+            store(m)

@@ -1,6 +1,7 @@
 from contextlib import ExitStack
 
 import concourse.mybir as mybir
+from concourse.masks import make_identity
 
 K, M, T, S = 512, 1024, 1024, 512
 P = 128
@@ -26,7 +27,8 @@ def tile_list_hboth_gelu_kernel(tc, xT, w_words, w_scales, wgt, b, wgo, offs, of
     with ExitStack() as ctx:
         lists = ctx.enter_context(tc.tile_pool(name="lists", bufs=1))
         keep = ctx.enter_context(tc.tile_pool(name="keep", bufs=1))
-        psum = ctx.enter_context(tc.psum_pool(name="psum", bufs=8))
+        psum = ctx.enter_context(tc.psum_pool(name="psum", bufs=6))
+        turn = ctx.enter_context(tc.psum_pool(name="turn", bufs=1))
 
         picks = lists.tile([P, S // 16], U16, name="picks")
         places = lists.tile([P, S // 16], U16, name="places")
@@ -35,14 +37,17 @@ def tile_list_hboth_gelu_kernel(tc, xT, w_words, w_scales, wgt, b, wgo, offs, of
         w_codes = keep.tile([P, 2 * M], U8, name="w_codes", align_bytes=64)
         w_plane = keep.tile([P, M], U8, name="w_plane", align_bytes=64)
         wgo_all = keep.tile([P, S], F32, name="wgo_all")
-        b_rows = keep.tile([P, 32], F32, name="b_rows", align_bytes=64)
-        b_cols = keep.tile([P, 32], F32, name="b_cols", align_bytes=64)
+        b_rows = keep.tile([P, P], F32, name="b_rows")
+        b_cols = keep.tile([P, M_TILES], F32, name="b_cols")
+        identity = keep.tile([P, P], F32, name="identity")
+        b_turned = turn.tile([P, P], F32, name="b_turned")
         warm_in = keep.tile([P, 8], F32, name="warm_in")
         warm_out = keep.tile([P, 8], F32, name="warm_out")
         rows = [keep.tile([P, T], F32, name=f"rows{m}") for m in range(M_TILES)]
 
-        nc.vector.memset(w_plane[:].bitcast(I32), 0)
         nc.vector.memset(b_rows[:], 0.0)
+        nc.scalar.dma_start(out=b_rows[0:M_TILES, :], in_=b.rearrange("(m p) -> m p", p=P))
+        nc.gpsimd.memset(w_plane[:].bitcast(I32), 0)
         nc.vector.memset(warm_in[:], 0.0)
         nc.scalar.activation(warm_out[:], warm_in[:], GELU)
 
@@ -53,45 +58,47 @@ def tile_list_hboth_gelu_kernel(tc, xT, w_words, w_scales, wgt, b, wgo, offs, of
         nc.sync.dma_start(out=wgt_half[1][:], in_=wgt[:, HALF:S])
         for i in range(1, PACK):
             nc.sync.dma_start(out=planes[i][:], in_=x_planes[:, i, :])
+        nc.sync.dma_start(out=w_codes[:].bitcast(I32), in_=w_words[0].bitcast(I32))
         for q in range(4):
-            nc.scalar.dma_start(
+            nc.sync.dma_start(
                 out=w_plane[32 * q : 32 * q + 4, :].bitcast(I32),
                 in_=w_scales[0, 4 * q : 4 * q + 4, :].bitcast(I32),
             )
-        b_view = b.rearrange("(m q c) -> q m c", q=4, c=32)
-        for q in range(4):
-            nc.scalar.dma_start(out=b_rows[32 * q : 32 * q + M_TILES, :], in_=b_view[q])
-        nc.sync.dma_start(out=w_codes[:].bitcast(I32), in_=w_words[0].bitcast(I32))
+        make_identity(nc, identity[:])
+        nc.tensor.transpose(b_turned[:], b_rows[:], identity[:])
         nc.sync.dma_start(places[:], offs2)
         nc.sync.dma_start(out=wgo_all[:], in_=wgo)
 
         for m in range(M_TILES):
-            if m < 5:
-                nc.vector.memset(rows[m][:], 0.0)
+            if m < 2:
+                nc.vector.memset(rows[m][:].bitcast(I32), 0)
             else:
-                nc.gpsimd.memset(rows[m][:], 0.0)
-        nc.vector.transpose(b_cols[:], b_rows[:])
+                nc.gpsimd.memset(rows[m][:].bitcast(I32), 0)
 
         codes = keep.tile([P, S], U32, name="codes", align_bytes=64)
         scales = keep.tile([P, S], U8, name="scales", align_bytes=64)
-        picked = [keep.tile([P, PACK, HALF], F32, name=f"picked{h}") for h in range(2)]
         grouped = [keep.tile([P, HALF, PACK], BF16, name=f"grouped{h}", align_bytes=64) for h in range(2)]
-        results = [[keep.tile([P, HALF], F32, name=f"res{m}_{h}") for h in range(2)] for m in range(M_TILES)]
+        picked = {}
+        results = [keep.tile([P, S], F32, name=f"result{m}") for m in range(M_TILES)]
 
-        def gather(h):
-            lo = h * HALF // 16
-            for i in range(PACK):
-                nc.vector.tensor_tensor(
-                    picked[h][:, i, :],
-                    planes[i][:].indirect(picks[:, lo : lo + HALF // 16]),
-                    wgt_half[h][:],
-                    MULT,
-                )
-                if i % 2 == 1:
-                    nc.scalar.copy(
-                        out=grouped[h][:, :, i - 1 : i + 1],
-                        in_=picked[h][:, i - 1 : i + 1, :].rearrange("p t c -> p c t"),
-                    )
+        def half_list(tile, h):
+            return tile[:, h * HALF // 16 : (h + 1) * HALF // 16]
+
+        def gather(h, i):
+            if i % 2 == 0:
+                picked[h, i // 2] = keep.tile([P, 2, HALF], F32, name="picked_late" if i == 2 else f"picked{h}")
+            nc.vector.tensor_tensor(
+                picked[h, i // 2][:, i % 2, :],
+                planes[i][:].indirect(half_list(picks, h)),
+                wgt_half[h][:],
+                MULT,
+            )
+
+        def group(copy, h, pair):
+            copy(
+                out=grouped[h][:, :, 2 * pair : 2 * pair + 2],
+                in_=picked[h, pair][:].rearrange("p t c -> p c t"),
+            )
 
         def quantize(h):
             cols = slice(h * HALF, (h + 1) * HALF)
@@ -101,9 +108,9 @@ def tile_list_hboth_gelu_kernel(tc, xT, w_words, w_scales, wgt, b, wgo, offs, of
                 in_=grouped[h][:].rearrange("p c t -> p (c t)"),
             )
 
-        def project(m, h):
-            cols = slice(h * HALF, (h + 1) * HALF)
-            acc = psum.tile([P, HALF], F32, name="acc")
+        def project(m, first, width):
+            cols = slice(first, first + width)
+            acc = psum.tile([P, width], F32, name="acc")
             nc.tensor.matmul_mx(
                 out=acc[:],
                 lhsT=w_codes[:, 2 * P * m : 2 * P * (m + 1)].bitcast(FP4X4),
@@ -113,11 +120,13 @@ def tile_list_hboth_gelu_kernel(tc, xT, w_words, w_scales, wgt, b, wgo, offs, of
                 start=True,
                 stop=True,
             )
-            nc.scalar.activation(results[m][h][:], acc[:], GELU, bias=b_cols[:, m : m + 1])
-            lo = h * HALF // 16
+            nc.scalar.activation(results[m][:, cols], acc[:], GELU, bias=b_cols[:, m : m + 1])
+
+        def place(m, h):
+            cols = slice(h * HALF, (h + 1) * HALF)
             nc.vector.tensor_tensor(
-                rows[m][:].indirect(places[:, lo : lo + HALF // 16]),
-                results[m][h][:],
+                rows[m][:].indirect(half_list(places, h)),
+                results[m][:, cols],
                 wgo_all[:, cols],
                 MULT,
             )
@@ -125,14 +134,37 @@ def tile_list_hboth_gelu_kernel(tc, xT, w_words, w_scales, wgt, b, wgo, offs, of
         def store(m):
             nc.sync.dma_start(out=out[P * m : P * (m + 1), :], in_=rows[m][:])
 
-        gather(0)
+        vcopy, scopy = nc.vector.tensor_copy, nc.scalar.copy
+        gather(0, 0)
+        gather(1, 0)
+        gather(0, 1)
+        group(scopy, 0, 0)
+        gather(1, 1)
+        group(scopy, 1, 0)
+        nc.vector.tensor_copy(out=b_cols[:], in_=b_turned[:, 0:M_TILES])
+        gather(0, 2)
+        gather(0, 3)
+        group(vcopy, 0, 1)
         quantize(0)
-        project(0, 0)
-        gather(1)
+        gather(1, 2)
+        project(0, 0, HALF)
+        gather(1, 3)
+        group(scopy, 1, 1)
+        project(1, 0, HALF)
+        place(0, 0)
         quantize(1)
-        project(1, 0)
-        for m in range(M_TILES):
-            if m >= 2:
-                project(m, 0)
-            project(m, 1)
+        place(1, 0)
+        project(0, HALF, HALF)
+        project(1, HALF, HALF)
+        place(0, 1)
+        store(0)
+        place(1, 1)
+        store(1)
+        for m in range(2, M_TILES, 2):
+            project(m, 0, S)
+            project(m + 1, 0, S)
+            for h in range(2):
+                place(m, h)
+                place(m + 1, h)
             store(m)
+            store(m + 1)

@@ -86,7 +86,7 @@ def tile_list_hboth_gelu_kernel(tc, xT, w_words, w_scales, wgt, b, wgo, offs, of
 
         def gather(h, i):
             if i % 2 == 0:
-                picked[h, i // 2] = keep.tile([P, 2, HALF], F32, name="picked_late" if i == 2 else f"picked{h}")
+                picked[h, i // 2] = keep.tile([P, 2, HALF], F32, name=f"picked{h}{i // 2}")
             nc.vector.tensor_tensor(
                 picked[h, i // 2][:, i % 2, :],
                 planes[i][:].indirect(half_list(picks, h)),
@@ -143,16 +143,16 @@ def tile_list_hboth_gelu_kernel(tc, xT, w_words, w_scales, wgt, b, wgo, offs, of
         group(scopy, 1, 0)
         nc.vector.tensor_copy(out=b_cols[:], in_=b_turned[:, 0:M_TILES])
         gather(0, 2)
+        gather(1, 2)
         gather(0, 3)
         group(vcopy, 0, 1)
         quantize(0)
-        gather(1, 2)
         project(0, 0, HALF)
         gather(1, 3)
-        group(scopy, 1, 1)
+        group(vcopy, 1, 1)
+        quantize(1)
         project(1, 0, HALF)
         place(0, 0)
-        quantize(1)
         place(1, 0)
         project(0, HALF, HALF)
         project(1, HALF, HALF)

from contextlib import ExitStack

import concourse.mybir as mybir
from concourse.masks import make_identity

K, M, T, S = 512, 1024, 1024, 512
P = 128
PACK = 4
HALF = S // 2
M_TILES = M // P
FLOPS = 2 * K * M * S

F32 = mybir.dt.float32
BF16 = mybir.dt.bfloat16
I32 = mybir.dt.int32
U32 = mybir.dt.uint32
U16 = mybir.dt.uint16
U8 = mybir.dt.uint8
FP8X4 = mybir.dt.float8_e4m3fn_x4
FP4X4 = mybir.dt.float4_e2m1fn_x4
MULT = mybir.AluOpType.mult
GELU = mybir.ActivationFunctionType.Gelu_apprx_tanh


def tile_list_hboth_gelu_kernel(tc, xT, w_words, w_scales, wgt, b, wgo, offs, offs2, out):
    nc = tc.nc
    with ExitStack() as ctx:
        lists = ctx.enter_context(tc.tile_pool(name="lists", bufs=1))
        keep = ctx.enter_context(tc.tile_pool(name="keep", bufs=1))
        psum = ctx.enter_context(tc.psum_pool(name="psum", bufs=6))
        turn = ctx.enter_context(tc.psum_pool(name="turn", bufs=1))

        picks = lists.tile([P, S // 16], U16, name="picks")
        places = lists.tile([P, S // 16], U16, name="places")
        wgt_half = [keep.tile([P, HALF], F32, name=f"wgt{h}") for h in range(2)]
        planes = [keep.tile([P, T], F32, name=f"plane{i}") for i in range(PACK)]
        w_codes = keep.tile([P, 2 * M], U8, name="w_codes", align_bytes=64)
        w_plane = keep.tile([P, M], U8, name="w_plane", align_bytes=64)
        wgo_all = keep.tile([P, S], F32, name="wgo_all")
        b_rows = keep.tile([P, P], F32, name="b_rows")
        b_cols = keep.tile([P, M_TILES], F32, name="b_cols")
        identity = keep.tile([P, P], F32, name="identity")
        b_turned = turn.tile([P, P], F32, name="b_turned")
        warm_in = keep.tile([P, 8], F32, name="warm_in")
        warm_out = keep.tile([P, 8], F32, name="warm_out")
        rows = [keep.tile([P, T], F32, name=f"rows{m}") for m in range(M_TILES)]

        nc.vector.memset(b_rows[:], 0.0)
        nc.scalar.dma_start(out=b_rows[0:M_TILES, :], in_=b.rearrange("(m p) -> m p", p=P))
        nc.gpsimd.memset(w_plane[:].bitcast(I32), 0)
        nc.vector.memset(warm_in[:], 0.0)
        nc.scalar.activation(warm_out[:], warm_in[:], GELU)

        x_planes = xT.rearrange("(p i) t -> p i t", i=PACK)
        nc.sync.dma_start(picks[:], offs)
        nc.sync.dma_start(out=wgt_half[0][:], in_=wgt[:, 0:HALF])
        nc.sync.dma_start(out=planes[0][:], in_=x_planes[:, 0, :])
        nc.sync.dma_start(out=wgt_half[1][:], in_=wgt[:, HALF:S])
        for i in range(1, PACK):
            nc.sync.dma_start(out=planes[i][:], in_=x_planes[:, i, :])
        nc.sync.dma_start(out=w_codes[:].bitcast(I32), in_=w_words[0].bitcast(I32))
        for q in range(4):
            nc.sync.dma_start(
                out=w_plane[32 * q : 32 * q + 4, :].bitcast(I32),
                in_=w_scales[0, 4 * q : 4 * q + 4, :].bitcast(I32),
            )
        make_identity(nc, identity[:])
        nc.tensor.transpose(b_turned[:], b_rows[:], identity[:])
        nc.sync.dma_start(places[:], offs2)
        nc.sync.dma_start(out=wgo_all[:], in_=wgo)

        for m in range(M_TILES):
            if m < 2:
                nc.vector.memset(rows[m][:].bitcast(I32), 0)
            else:
                nc.gpsimd.memset(rows[m][:].bitcast(I32), 0)

        codes = keep.tile([P, S], U32, name="codes", align_bytes=64)
        scales = keep.tile([P, S], U8, name="scales", align_bytes=64)
        grouped = [keep.tile([P, HALF, PACK], BF16, name=f"grouped{h}", align_bytes=64) for h in range(2)]
        picked = {}
        results = [keep.tile([P, S], F32, name=f"result{m}") for m in range(M_TILES)]

        def half_list(tile, h):
            return tile[:, h * HALF // 16 : (h + 1) * HALF // 16]

        def gather(h, i):
            if i % 2 == 0:
                picked[h, i // 2] = keep.tile([P, 2, HALF], F32, name=f"picked{h}{i // 2}")
            nc.vector.tensor_tensor(
                picked[h, i // 2][:, i % 2, :],
                planes[i][:].indirect(half_list(picks, h)),
                wgt_half[h][:],
                MULT,
            )

        def group(copy, h, pair):
            copy(
                out=grouped[h][:, :, 2 * pair : 2 * pair + 2],
                in_=picked[h, pair][:].rearrange("p t c -> p c t"),
            )

        def quantize(h):
            cols = slice(h * HALF, (h + 1) * HALF)
            nc.vector.quantize_mx(
                out=codes[:, cols].bitcast(FP8X4),
                scales=scales[:, cols],
                in_=grouped[h][:].rearrange("p c t -> p (c t)"),
            )

        def project(m, first, width):
            cols = slice(first, first + width)
            acc = psum.tile([P, width], F32, name="acc")
            nc.tensor.matmul_mx(
                out=acc[:],
                lhsT=w_codes[:, 2 * P * m : 2 * P * (m + 1)].bitcast(FP4X4),
                lhsT_scale=w_plane[:, P * m : P * (m + 1)],
                rhs=codes[:, cols].bitcast(FP8X4),
                rhs_scale=scales[:, cols],
                start=True,
                stop=True,
            )
            nc.scalar.activation(results[m][:, cols], acc[:], GELU, bias=b_cols[:, m : m + 1])

        def place(m, h):
            cols = slice(h * HALF, (h + 1) * HALF)
            nc.vector.tensor_tensor(
                rows[m][:].indirect(half_list(places, h)),
                results[m][:, cols],
                wgo_all[:, cols],
                MULT,
            )

        def store(m):
            nc.sync.dma_start(out=out[P * m : P * (m + 1), :], in_=rows[m][:])

        vcopy, scopy = nc.vector.tensor_copy, nc.scalar.copy
        gather(0, 0)
        gather(1, 0)
        gather(0, 1)
        group(scopy, 0, 0)
        gather(1, 1)
        group(scopy, 1, 0)
        nc.vector.tensor_copy(out=b_cols[:], in_=b_turned[:, 0:M_TILES])
        gather(0, 2)
        gather(1, 2)
        gather(0, 3)
        group(vcopy, 0, 1)
        quantize(0)
        project(0, 0, HALF)
        gather(1, 3)
        group(vcopy, 1, 1)
        quantize(1)
        project(1, 0, HALF)
        place(0, 0)
        place(1, 0)
        project(0, HALF, HALF)
        project(1, HALF, HALF)
        place(0, 1)
        store(0)
        place(1, 1)
        store(1)
        for m in range(2, M_TILES, 2):
            project(m, 0, S)
            project(m + 1, 0, S)
            for h in range(2):
                place(m, h)
                place(m + 1, h)
            store(m)
            store(m + 1)
